import numpy as np
import ml_dtypes


def mxq(x, axis, fmt="e4m3"):
    dtype, down = {"e4m3": (ml_dtypes.float8_e4m3fn, 7), "e5m2": (ml_dtypes.float8_e5m2, 14)}[fmt]
    v = np.moveaxis(np.asarray(x, np.float32).astype(ml_dtypes.bfloat16).astype(np.float64), axis, -1)
    blocks = v.reshape(v.shape[:-1] + (-1, 32))
    amax = np.abs(blocks).max(-1, keepdims=True)
    byte = np.maximum(np.where(amax > 0, np.frexp(amax)[1] - 1 + 127, 0) - down, 1)
    scale = np.exp2(byte - 127.0)
    codes = (blocks / scale).astype(np.float32).astype(dtype).astype(np.float64)
    return np.moveaxis((codes * scale).reshape(v.shape), -1, axis)


WIDE = False


def mx_kscale(k):
    if not WIDE:
        return np.ones(k)
    levels = np.array([10, -10, 5, -5, 0])
    if k % 512:
        return np.exp2(np.random.permutation(np.resize(levels, k // 32))).repeat(32)
    a = np.empty((k // 512, 16))
    for p in range(k // 512):
        a[p, :8] = np.random.permutation(np.resize(levels, 8))
        for g in range(8):
            far = levels[np.abs(levels - a[p, g]) >= 10]
            a[p, g + 8] = far[np.random.randint(len(far))]
    return np.exp2(a.ravel()).repeat(32)


def f64(x):
    return np.asarray(x).astype(np.float64)


def striped(idx):
    return np.tile(idx.reshape(-1, 16).T, (8, 1)).astype(np.uint16)


def unstriped(offs):
    return offs[:16].T.reshape(-1).astype(np.int64)


def pack_weight(w):
    k, n = w.shape
    w = f64(np.asarray(w, np.float32).astype(ml_dtypes.bfloat16)).reshape(k // 32, 32, n)
    amax = np.abs(w).max(1)
    byte = np.clip(np.where(amax > 0, np.frexp(amax)[1] - 1 + 127 - 7, 1), 1, 254)
    scaled = (w * np.exp2(127.0 - byte)[:, None, :]).reshape(k, n).astype(np.float32)
    words = np.ascontiguousarray(scaled.reshape(k // 512, 128, 4, n).transpose(0, 1, 3, 2)).astype(ml_dtypes.float8_e4m3fn).view(np.uint8)
    return words, np.ascontiguousarray(byte.astype(np.uint8).reshape(k // 512, 16, n))


def unpack_weight(words, scales):
    g, p, n, _ = words.shape
    vals = np.ascontiguousarray(words).view(ml_dtypes.float8_e4m3fn).astype(np.float64) * np.repeat(np.exp2(scales.astype(np.float64) - 127.0), 8, axis=1)[..., None]
    return vals.transpose(0, 1, 3, 2).reshape(g * 512, n)


E2M1 = np.array([0.0, 0.5, 1.0, 1.5, 2.0, 3.0, 4.0, 6.0, -0.0, -0.5, -1.0, -1.5, -2.0, -3.0, -4.0, -6.0])


def pack_fp4(w):
    k, n = w.shape
    w = f64(np.asarray(w, np.float32).astype(ml_dtypes.bfloat16)).reshape(k // 32, 32, n)
    amax = np.abs(w).max(1)
    mant, ex = np.frexp(amax / 6.0)
    byte = np.clip(np.where(amax > 0, np.where(mant > 0.5, ex, ex - 1) + 127, 1), 1, 254)
    scaled = (w * np.exp2(127.0 - byte)[:, None, :]).reshape(k, n).astype(np.float32)
    c = np.ascontiguousarray(scaled.reshape(k // 512, 128, 4, n).transpose(0, 1, 3, 2)).astype(ml_dtypes.float4_e2m1fn).view(np.uint8) & 0xF
    words = (c[..., 0::2] | (c[..., 1::2] << 4)).reshape(k // 512, 128, 2 * n)
    return np.ascontiguousarray(words), np.ascontiguousarray(byte.astype(np.uint8).reshape(k // 512, 16, n))


def unpack_fp4(words, scales):
    g, _, n = scales.shape
    words = np.ascontiguousarray(words).reshape(g, 128, n, 2)
    nib = np.empty((g, 128, n, 4), np.uint8)
    nib[..., 0::2] = words & 0xF
    nib[..., 1::2] = words >> 4
    vals = E2M1[nib] * np.repeat(np.exp2(scales.astype(np.float64) - 127.0), 8, axis=1)[..., None]
    return vals.transpose(0, 1, 3, 2).reshape(g * 512, n)


K, T, S, N, H = 1024, 1024, 512, 256, 512


def setup_inputs():
    n = np.random.standard_normal
    s = mx_kscale(K)[:, None]
    u = mx_kscale(H)
    packed_xT = pack_weight(n((K, T)) * s)
    packed_w1 = pack_fp4(n((K, H)) / np.sqrt(K) / s)
    packed_w2 = pack_fp4(n((K, H)) / np.sqrt(K) / s)
    packed_w3 = pack_fp4(n((H, N)) / np.sqrt(H) / u[:, None])
    return {
        "x_words": packed_xT[0],
        "x_scales": packed_xT[1],
        "w1_words": packed_w1[0],
        "w1_scales": packed_w1[1],
        "w2_words": packed_w2[0],
        "w2_scales": packed_w2[1],
        "ph": (np.random.uniform(-1.0, 1.0, (H, S))).astype(np.float32),
        "goal": (n((H, S))).astype(np.float32),
        "unit": (np.random.uniform(0.6, 1.4, (H, 1)) * u[:, None]).astype(np.float32),
        "w3_words": packed_w3[0],
        "w3_scales": packed_w3[1],
        "offs": striped(np.random.permutation(T)[:S]),
        "phs": striped(np.random.permutation(S)),
    }


def reference(x_words, x_scales, w1_words, w1_scales, w2_words, w2_scales, ph, goal, unit, w3_words, w3_scales, offs, phs):
    xq = unpack_weight(x_words, x_scales)[:, unstriped(offs)]
    ww = unpack_fp4(w2_words, w2_scales).T @ xq
    ctr = np.tanh(ww)
    psi = np.exp(-1.0 * ((ctr - f64(ph)) ** 2))
    y = unpack_fp4(w1_words, w1_scales).T @ xq
    mps = psi.mean(axis=1, keepdims=True)
    force = (psi * y) / (mps + 0.2)
    fp = force[:, unstriped(phs)]
    acc_ = force + f64(goal) - (0.6 * fp)
    vel = acc_ / (np.abs(acc_) + 1.0)
    pp = psi[:, unstriped(phs)]
    hid = f64(unit) * (vel * pp)
    return unpack_fp4(w3_words, w3_scales).T @ mxq(hid, 0, "e4m3")

@@ -1,0 +1,202 @@
+from contextlib import ExitStack
+
+import concourse.mybir as mybir
+
+K, T, S, N, H = 1024, 1024, 512, 256, 512
+FLOPS = 2 * S * (2 * K * H + H * N)
+
+F32 = mybir.dt.float32
+BF16 = mybir.dt.bfloat16
+I32 = mybir.dt.int32
+U32 = mybir.dt.uint32
+U16 = mybir.dt.uint16
+U8 = mybir.dt.uint8
+FP8X4 = mybir.dt.float8_e4m3fn_x4
+FP4X4 = mybir.dt.float4_e2m1fn_x4
+ACT = mybir.ActivationFunctionType
+ALU = mybir.AluOpType
+
+P = 128
+PACK = 4
+PASSES = K // (P * PACK)
+CHUNKS = (256, 128, 128)
+FUSED_TILES = 1
+DAMP = 0.6
+
+
+def load_scales(queue, plane, scales):
+    passes = scales.shape[0]
+    rows = plane[:].bitcast(I32).rearrange("p (o n) -> p o n", o=passes)
+    for q in range(4):
+        queue.dma_start(
+            out=rows[32 * q : 32 * q + 4],
+            in_=scales[:, 4 * q : 4 * q + 4, :].bitcast(I32).rearrange("o r n -> r o n"),
+        )
+
+
+def tile_picked_ydmpob_psi_p_kernel(
+    tc, x_words, x_scales, w1_words, w1_scales, w2_words, w2_scales, ph, goal, unit, w3_words, w3_scales, offs, phs, out
+):
+    nc = tc.nc
+    with ExitStack() as ctx:
+        keep = ctx.enter_context(tc.tile_pool(name="keep", bufs=1))
+        psum = ctx.enter_context(tc.psum_pool(name="psum", bufs=1))
+
+        def sb(shape, dtype, name, tag=None):
+            return keep.tile(shape, dtype, name=name, tag=tag or name, align_bytes=64)
+
+        offs_t = keep.tile([P, S // 16], U16, name="offs_t")
+        phs_t = keep.tile([P, S // 16], U16, name="phs_t")
+        xs = sb([P, PASSES * T], U8, "xs")
+        w2s_raw = sb([P, PASSES * H], U8, "w2s_raw")
+        w1s_raw = sb([P, PASSES * H], U8, "w1s_raw")
+        w3s = sb([P, N], U8, "w3s")
+        one = sb([P, 1], F32, "one")
+        nc.gpsimd.memset(xs[:].bitcast(I32), 0)
+        for plane in (w2s_raw, w1s_raw, w3s):
+            nc.vector.memset(plane[:].bitcast(I32), 0)
+        nc.vector.memset(one[:], 1.0)
+
+        xw = [sb([P, T], U32, f"xw{o}") for o in range(PASSES)]
+        w2_raw = sb([P, PASSES * 2 * H], U8, "w2_raw")
+        w1_raw = sb([P, PASSES * 2 * H], U8, "w1_raw")
+        w3w = sb([P, 2 * N], U8, "w3w")
+        ph_t = sb([P, PACK, S], F32, "ph_t")
+        goal_t = sb([P, PACK, S], F32, "goal_t")
+        unit_t = sb([P, PACK], F32, "unit_t")
+
+        def load_words(queue, raw, words):
+            queue.dma_start(
+                out=raw[:].bitcast(I32).rearrange("p (o n) -> p o n", o=words.shape[0]),
+                in_=words.bitcast(I32).rearrange("o p n -> p o n"),
+            )
+
+        def load_x(o):
+            nc.sync.dma_start(out=xw[o][:].bitcast(I32), in_=x_words[o].rearrange("p c r -> p (c r)").bitcast(I32))
+
+        nc.sync.dma_start(offs_t[:], offs)
+        load_scales(nc.sync, xs, x_scales)
+        load_x(0)
+        load_x(1)
+        load_words(nc.sync, w2_raw, w2_words)
+        load_scales(nc.sync, w2s_raw, w2_scales)
+        load_words(nc.sync, w1_raw, w1_words)
+        nc.sync.dma_start(out=ph_t[:], in_=ph.rearrange("(p t) j -> p t j", t=PACK))
+        load_scales(nc.sync, w1s_raw, w1_scales)
+        nc.sync.dma_start(out=goal_t[:], in_=goal.rearrange("(p t) j -> p t j", t=PACK))
+        nc.sync.dma_start(phs_t[:], phs)
+        nc.sync.dma_start(out=unit_t[:], in_=unit.rearrange("(p t) o -> p (t o)", t=PACK))
+        load_words(nc.sync, w3w, w3_words)
+        load_scales(nc.sync, w3s, w3_scales)
+
+        def deal(words_raw, scales_raw, name, engine):
+            words = sb([P, PASSES * 2 * H], U8, name + "_words")
+            scales = sb([P, PASSES * H], U8, name + "_scales")
+            nc.scalar.copy(
+                out=words[:].bitcast(U16).rearrange("p (o t m) -> p o t m", o=PASSES, t=PACK),
+                in_=words_raw[:].bitcast(U16).rearrange("p (o m t) -> p o t m", o=PASSES, t=PACK),
+            )
+            engine.tensor_copy(
+                out=scales[:].rearrange("p (o t m) -> p o t m", o=PASSES, t=PACK),
+                in_=scales_raw[:].rearrange("p (o m t) -> p o t m", o=PASSES, t=PACK),
+            )
+            return words, scales
+
+        gw = [sb([P, S], U32, f"gw{o}") for o in range(PASSES)]
+        gs = [sb([P, S], U8, f"gs{o}") for o in range(PASSES)]
+        for o in range(PASSES):
+            nc.vector.tensor_copy(out=gs[o][:], in_=xs[:, o * T : (o + 1) * T].indirect(offs_t[:]))
+        w2w, w2s = deal(w2_raw, w2s_raw, "w2", nc.vector)
+        for o in range(PASSES):
+            nc.vector.tensor_copy(out=gw[o][:], in_=xw[o][:].indirect(offs_t[:]))
+        w1w, w1s = deal(w1_raw, w1s_raw, "w1", nc.gpsimd)
+
+        def product(bank, words, scales, t):
+            for o in range(PASSES):
+                c0 = o * H + t * P
+                nc.tensor.matmul_mx(
+                    out=bank[:],
+                    lhsT=words[:, 2 * c0 : 2 * (c0 + P)].bitcast(FP4X4),
+                    lhsT_scale=scales[:, c0 : c0 + P],
+                    rhs=gw[o][:].bitcast(FP8X4),
+                    rhs_scale=gs[o][:],
+                    start=(o == 0),
+                    stop=(o == PASSES - 1),
+                )
+
+        sq = sb([P, PACK, S], F32, "sq", tag="sq_or_root")
+        psi, y, damp = [], [], []
+        for t in range(PACK):
+            ww = psum.tile([P, S], F32, name="ww", tag="ww", bufs=2)
+            product(ww, w2w, w2s, t)
+            ctr = sb([P, S], F32, f"ctr{t}")
+            nc.scalar.activation(ctr[:], ww[:], ACT.Tanh)
+            dist = sb([P, S], F32, f"dist{t}")
+            nc.vector.tensor_tensor(dist[:], ctr[:], ph_t[:, t, :], ALU.subtract)
+            nc.scalar.activation(sq[:, t, :], dist[:], ACT.Square)
+            psi_t = sb([P, S + 1], F32, f"psi{t}")
+            nc.scalar.activation(psi_t[:, :S], sq[:, t, :], ACT.Exp, scale=-1.0, accum_out=psi_t[:, S:])
+            den = sb([P, 1], F32, f"den{t}")
+            nc.scalar.activation(den[:], psi_t[:, S:], ACT.Copy, scale=-1.0 / (DAMP * S), bias=-0.2 / DAMP)
+            damp_t = sb([P, S + 1], F32, f"damp{t}")
+            nc.vector.reciprocal(damp_t[:, S:], den[:])
+            y_t = psum.tile([P, S], F32, name=f"y{t}", tag=f"y{t}")
+            product(y_t, w1w, w1s, t)
+            psi.append(psi_t)
+            y.append(y_t)
+            damp.append(damp_t)
+
+        acc = [sb([P, S], F32, f"acc{t}") for t in range(PACK)]
+        for t in range(PACK):
+            nc.vector.scalar_tensor_tensor(damp[t][:, :S], y[t][:], damp[t][:, S:], psi[t][:, :S], ALU.mult, ALU.mult)
+            pull = sb([P, S], F32, f"pull{t}")
+            nc.vector.scalar_tensor_tensor(pull[:], damp[t][:, :S], -1.0 / DAMP, goal_t[:, t, :], ALU.mult, ALU.add)
+            nc.vector.tensor_tensor(acc[t][:], damp[t][:].indirect(phs_t[:]), pull[:], ALU.add)
+
+        root = sb([P, PACK, S], F32, "root", tag="sq_or_root")
+        left = sb([P, PACK, S], F32, "left")
+        right = sb([P, PACK, S], F32, "right")
+        for t in range(PACK):
+            mag = sb([P, S], F32, f"mag{t}")
+            nc.scalar.activation(mag[:], acc[t][:], ACT.Abs)
+            if t < FUSED_TILES:
+                nc.scalar.activation(root[:, t, :], mag[:], ACT.Abs_reciprocal_sqrt, bias=one[:])
+            else:
+                mag2 = sb([P, S], F32, f"mag2{t}")
+                nc.scalar.activation(mag2[:], mag[:], ACT.Square, bias=one[:])
+                nc.scalar.activation(root[:, t, :], mag2[:], ACT.Abs_reciprocal_sqrt)
+            nc.vector.scalar_tensor_tensor(left[:, t, :], acc[t][:], unit_t[:, t : t + 1], root[:, t, :], ALU.mult, ALU.mult)
+            if t < FUSED_TILES:
+                nc.vector.tensor_tensor(right[:, t, :], psi[t][:].indirect(phs_t[:]), root[:, t, :], ALU.mult)
+        for t in range(FUSED_TILES, PACK):
+            nc.scalar.activation(right[:, t, :], psi[t][:].indirect(phs_t[:]), ACT.Copy)
+
+        out_v = out.rearrange("(mt p) j -> p mt j", p=P)
+        j0 = 0
+        for c, width in enumerate(CHUNKS):
+            cols = slice(j0, j0 + width)
+            j0 = j0 + width
+            hid = sb([P, width * PACK], BF16, f"hid{c}")
+            nc.vector.tensor_tensor(
+                hid[:].rearrange("p (g i t) -> p g t i", i=4, t=PACK),
+                left[:, :, cols].rearrange("p t (g i) -> p g t i", i=4),
+                right[:, :, cols].rearrange("p t (g i) -> p g t i", i=4),
+                ALU.mult,
+            )
+            codes = sb([P, width], U32, f"codes{c}")
+            plane = sb([P, width], U8, f"plane{c}")
+            nc.vector.quantize_mx(out=codes[:].bitcast(FP8X4), scales=plane[:], in_=hid[:])
+            joints = psum.tile([P, N // P, width], F32, name="joints", tag="joints", bufs=2)
+            for mt in range(N // P):
+                nc.tensor.matmul_mx(
+                    out=joints[:, mt, :],
+                    lhsT=w3w[:, 2 * mt * P : 2 * (mt + 1) * P].bitcast(FP4X4),
+                    lhsT_scale=w3s[:, mt * P : (mt + 1) * P],
+                    rhs=codes[:].bitcast(FP8X4),
+                    rhs_scale=plane[:],
+                    start=True,
+                    stop=True,
+                )
+            res = sb([P, N // P, width], F32, f"res{c}")
+            nc.scalar.copy(res[:], joints[:])
+            nc.sync.dma_start(out=out_v[:, :, cols], in_=res[:])

@@ -19,16 +19,17 @@ ALU = mybir.AluOpType
 P = 128
 PACK = 4
 PASSES = K // (P * PACK)
-CHUNKS = (256, 128, 128)
-FUSED_TILES = 1
+CHUNKS = ((0, 0, 256), (1, 0, 128), (1, 128, 128))
+FUSED = ((0, 0),)
+HALF = S // 2
 DAMP = 0.6
 
 
-def load_scales(queue, plane, scales):
+def load_scales(queues, plane, scales):
     passes = scales.shape[0]
     rows = plane[:].bitcast(I32).rearrange("p (o n) -> p o n", o=passes)
     for q in range(4):
-        queue.dma_start(
+        queues[q].dma_start(
             out=rows[32 * q : 32 * q + 4],
             in_=scales[:, 4 * q : 4 * q + 4, :].bitcast(I32).rearrange("o r n -> r o n"),
         )
@@ -75,19 +76,19 @@ def tile_picked_ydmpob_psi_p_kernel(
             nc.sync.dma_start(out=xw[o][:].bitcast(I32), in_=x_words[o].rearrange("p c r -> p (c r)").bitcast(I32))
 
         nc.sync.dma_start(offs_t[:], offs)
-        load_scales(nc.sync, xs, x_scales)
         load_x(0)
+        load_scales([nc.sync] * 4, xs, x_scales)
         load_x(1)
         load_words(nc.sync, w2_raw, w2_words)
-        load_scales(nc.sync, w2s_raw, w2_scales)
-        load_words(nc.sync, w1_raw, w1_words)
+        load_scales([nc.sync] * 4, w2s_raw, w2_scales)
         nc.sync.dma_start(out=ph_t[:], in_=ph.rearrange("(p t) j -> p t j", t=PACK))
-        load_scales(nc.sync, w1s_raw, w1_scales)
+        load_words(nc.sync, w1_raw, w1_words)
+        load_scales([nc.sync] * 4, w1s_raw, w1_scales)
         nc.sync.dma_start(out=goal_t[:], in_=goal.rearrange("(p t) j -> p t j", t=PACK))
         nc.sync.dma_start(phs_t[:], phs)
         nc.sync.dma_start(out=unit_t[:], in_=unit.rearrange("(p t) o -> p (t o)", t=PACK))
         load_words(nc.sync, w3w, w3_words)
-        load_scales(nc.sync, w3s, w3_scales)
+        load_scales([nc.sync] * 4, w3s, w3_scales)
 
         def deal(words_raw, scales_raw, name, engine):
             words = sb([P, PASSES * 2 * H], U8, name + "_words")
@@ -96,97 +97,138 @@ def tile_picked_ydmpob_psi_p_kernel(
                 out=words[:].bitcast(U16).rearrange("p (o t m) -> p o t m", o=PASSES, t=PACK),
                 in_=words_raw[:].bitcast(U16).rearrange("p (o m t) -> p o t m", o=PASSES, t=PACK),
             )
-            engine.tensor_copy(
-                out=scales[:].rearrange("p (o t m) -> p o t m", o=PASSES, t=PACK),
-                in_=scales_raw[:].rearrange("p (o m t) -> p o t m", o=PASSES, t=PACK),
-            )
+            for o in range(PASSES):
+                engine.tensor_copy(
+                    out=scales[:, o * H : (o + 1) * H].rearrange("p (t m) -> p t m", t=PACK),
+                    in_=scales_raw[:, o * H : (o + 1) * H].rearrange("p (m t) -> p t m", t=PACK),
+                )
             return words, scales
 
         gw = [sb([P, S], U32, f"gw{o}") for o in range(PASSES)]
         gs = [sb([P, S], U8, f"gs{o}") for o in range(PASSES)]
-        for o in range(PASSES):
-            nc.vector.tensor_copy(out=gs[o][:], in_=xs[:, o * T : (o + 1) * T].indirect(offs_t[:]))
-        w2w, w2s = deal(w2_raw, w2s_raw, "w2", nc.vector)
-        for o in range(PASSES):
-            nc.vector.tensor_copy(out=gw[o][:], in_=xw[o][:].indirect(offs_t[:]))
+
+        def half(h):
+            return slice(h * HALF, (h + 1) * HALF)
+
+        def pick(h):
+            entries = offs_t[:, h * HALF // 16 : (h + 1) * HALF // 16]
+            for o in range(PASSES):
+                nc.vector.tensor_copy(out=gs[o][:, half(h)], in_=xs[:, o * T : (o + 1) * T].indirect(entries))
+            for o in range(PASSES):
+                nc.vector.tensor_copy(out=gw[o][:, half(h)], in_=xw[o][:].indirect(entries))
+
+        pick(0)
+        w2w, w2s = deal(w2_raw, w2s_raw, "w2", nc.gpsimd)
+        pick(1)
         w1w, w1s = deal(w1_raw, w1s_raw, "w1", nc.gpsimd)
 
-        def product(bank, words, scales, t):
+        def product(bank, words, scales, t, cols):
             for o in range(PASSES):
                 c0 = o * H + t * P
                 nc.tensor.matmul_mx(
-                    out=bank[:],
+                    out=bank,
                     lhsT=words[:, 2 * c0 : 2 * (c0 + P)].bitcast(FP4X4),
                     lhsT_scale=scales[:, c0 : c0 + P],
-                    rhs=gw[o][:].bitcast(FP8X4),
-                    rhs_scale=gs[o][:],
+                    rhs=gw[o][:, cols].bitcast(FP8X4),
+                    rhs_scale=gs[o][:, cols],
                     start=(o == 0),
                     stop=(o == PASSES - 1),
                 )
 
         sq = sb([P, PACK, S], F32, "sq", tag="sq_or_root")
         psi, y, damp = [], [], []
-        for t in range(PACK):
-            ww = psum.tile([P, S], F32, name="ww", tag="ww", bufs=2)
-            product(ww, w2w, w2s, t)
-            ctr = sb([P, S], F32, f"ctr{t}")
+
+        def distance(pair, h):
+            rows = slice(2 * pair, 2 * pair + 2)
+            ww = psum.tile([P, 2, HALF], F32, name="ww", tag="short", bufs=4)
+            for u in range(2):
+                product(ww[:, u, :], w2w, w2s, 2 * pair + u, half(h))
+            ctr = sb([P, 2, HALF], F32, f"ctr{pair}{h}")
             nc.scalar.activation(ctr[:], ww[:], ACT.Tanh)
-            dist = sb([P, S], F32, f"dist{t}")
-            nc.vector.tensor_tensor(dist[:], ctr[:], ph_t[:, t, :], ALU.subtract)
-            nc.scalar.activation(sq[:, t, :], dist[:], ACT.Square)
+            dist = sb([P, 2, HALF], F32, f"dist{pair}{h}")
+            nc.vector.tensor_tensor(dist[:], ctr[:], ph_t[:, rows, half(h)], ALU.subtract)
+            if pair == 0:
+                nc.vector.tensor_tensor(sq[:, rows, half(h)], dist[:], dist[:], ALU.mult)
+            else:
+                nc.scalar.activation(sq[:, rows, half(h)], dist[:], ACT.Square)
+
+        def gauss(t):
             psi_t = sb([P, S + 1], F32, f"psi{t}")
             nc.scalar.activation(psi_t[:, :S], sq[:, t, :], ACT.Exp, scale=-1.0, accum_out=psi_t[:, S:])
             den = sb([P, 1], F32, f"den{t}")
-            nc.scalar.activation(den[:], psi_t[:, S:], ACT.Copy, scale=-1.0 / (DAMP * S), bias=-0.2 / DAMP)
+            nc.vector.tensor_scalar(den[:], psi_t[:, S:], -1.0 / (DAMP * S), -0.2 / DAMP, ALU.mult, ALU.add)
             damp_t = sb([P, S + 1], F32, f"damp{t}")
             nc.vector.reciprocal(damp_t[:, S:], den[:])
             y_t = psum.tile([P, S], F32, name=f"y{t}", tag=f"y{t}")
-            product(y_t, w1w, w1s, t)
+            product(y_t[:], w1w, w1s, t, slice(0, S))
             psi.append(psi_t)
             y.append(y_t)
             damp.append(damp_t)
 
-        acc = [sb([P, S], F32, f"acc{t}") for t in range(PACK)]
+        distance(0, 0)
+        distance(0, 1)
+        gauss(0)
+        gauss(1)
+        distance(1, 0)
+        distance(1, 1)
+        gauss(2)
+        gauss(3)
+
+        def places(h):
+            return phs_t[:, h * HALF // 16 : (h + 1) * HALF // 16]
+
+        acc = sb([P, 2, PACK, HALF], F32, "acc")
+        pull = [sb([P, S], F32, f"pull{t}") for t in range(PACK)]
         for t in range(PACK):
             nc.vector.scalar_tensor_tensor(damp[t][:, :S], y[t][:], damp[t][:, S:], psi[t][:, :S], ALU.mult, ALU.mult)
-            pull = sb([P, S], F32, f"pull{t}")
-            nc.vector.scalar_tensor_tensor(pull[:], damp[t][:, :S], -1.0 / DAMP, goal_t[:, t, :], ALU.mult, ALU.add)
-            nc.vector.tensor_tensor(acc[t][:], damp[t][:].indirect(phs_t[:]), pull[:], ALU.add)
-
-        root = sb([P, PACK, S], F32, "root", tag="sq_or_root")
-        left = sb([P, PACK, S], F32, "left")
-        right = sb([P, PACK, S], F32, "right")
+            nc.vector.scalar_tensor_tensor(pull[t][:], damp[t][:, :S], -1.0 / DAMP, goal_t[:, t, :], ALU.mult, ALU.add)
+            nc.vector.tensor_tensor(acc[:, 0, t, :], damp[t][:].indirect(places(0)), pull[t][:, half(0)], ALU.add)
         for t in range(PACK):
-            mag = sb([P, S], F32, f"mag{t}")
-            nc.scalar.activation(mag[:], acc[t][:], ACT.Abs)
-            if t < FUSED_TILES:
-                nc.scalar.activation(root[:, t, :], mag[:], ACT.Abs_reciprocal_sqrt, bias=one[:])
-            else:
-                mag2 = sb([P, S], F32, f"mag2{t}")
-                nc.scalar.activation(mag2[:], mag[:], ACT.Square, bias=one[:])
-                nc.scalar.activation(root[:, t, :], mag2[:], ACT.Abs_reciprocal_sqrt)
-            nc.vector.scalar_tensor_tensor(left[:, t, :], acc[t][:], unit_t[:, t : t + 1], root[:, t, :], ALU.mult, ALU.mult)
-            if t < FUSED_TILES:
-                nc.vector.tensor_tensor(right[:, t, :], psi[t][:].indirect(phs_t[:]), root[:, t, :], ALU.mult)
-        for t in range(FUSED_TILES, PACK):
-            nc.scalar.activation(right[:, t, :], psi[t][:].indirect(phs_t[:]), ACT.Copy)
+            nc.vector.tensor_tensor(acc[:, 1, t, :], damp[t][:].indirect(places(1)), pull[t][:, half(1)], ALU.add)
+
+        root = sb([P, 2, PACK, HALF], F32, "root", tag="sq_or_root")
+        mag = sb([P, 2, PACK, HALF], F32, "mag")
+        mag2 = sb([P, 2, PACK, HALF], F32, "mag2")
+        left = sb([P, 2, PACK, HALF], F32, "left")
+        right = sb([P, 2, PACK, HALF], F32, "right")
+
+        def saturate(h):
+            for pair in range(2):
+                rows = slice(2 * pair, 2 * pair + 2)
+                fused = (pair, h) in FUSED
+                nc.scalar.activation(mag[:, h, rows, :], acc[:, h, rows, :], ACT.Abs)
+                if fused:
+                    nc.scalar.activation(root[:, h, rows, :], mag[:, h, rows, :], ACT.Abs_reciprocal_sqrt, bias=one[:])
+                else:
+                    nc.scalar.activation(mag2[:, h, rows, :], mag[:, h, rows, :], ACT.Square, bias=one[:])
+                    nc.scalar.activation(root[:, h, rows, :], mag2[:, h, rows, :], ACT.Abs_reciprocal_sqrt)
+                for t in (2 * pair, 2 * pair + 1):
+                    nc.vector.scalar_tensor_tensor(
+                        left[:, h, t, :], acc[:, h, t, :], unit_t[:, t : t + 1], root[:, h, t, :], ALU.mult, ALU.mult
+                    )
+                    if fused:
+                        nc.vector.tensor_tensor(right[:, h, t, :], psi[t][:].indirect(places(h)), root[:, h, t, :], ALU.mult)
+            for t in range(PACK):
+                if (t // 2, h) not in FUSED:
+                    nc.scalar.activation(right[:, h, t, :], psi[t][:].indirect(places(h)), ACT.Copy)
 
         out_v = out.rearrange("(mt p) j -> p mt j", p=P)
-        j0 = 0
-        for c, width in enumerate(CHUNKS):
-            cols = slice(j0, j0 + width)
-            j0 = j0 + width
+        for c, (h, j0, width) in enumerate(CHUNKS):
+            if j0 == 0:
+                saturate(h)
+            inner = slice(j0, j0 + width)
+            cols = slice(h * HALF + j0, h * HALF + j0 + width)
             hid = sb([P, width * PACK], BF16, f"hid{c}")
             nc.vector.tensor_tensor(
                 hid[:].rearrange("p (g i t) -> p g t i", i=4, t=PACK),
-                left[:, :, cols].rearrange("p t (g i) -> p g t i", i=4),
-                right[:, :, cols].rearrange("p t (g i) -> p g t i", i=4),
+                left[:, h, :, inner].rearrange("p t (g i) -> p g t i", i=4),
+                right[:, h, :, inner].rearrange("p t (g i) -> p g t i", i=4),
                 ALU.mult,
             )
             codes = sb([P, width], U32, f"codes{c}")
             plane = sb([P, width], U8, f"plane{c}")
             nc.vector.quantize_mx(out=codes[:].bitcast(FP8X4), scales=plane[:], in_=hid[:])
-            joints = psum.tile([P, N // P, width], F32, name="joints", tag="joints", bufs=2)
+            joints = psum.tile([P, N // P, width], F32, name="joints", tag="short", bufs=4)
             for mt in range(N // P):
                 nc.tensor.matmul_mx(
                     out=joints[:, mt, :],

@@ -18,21 +18,43 @@ ALU = mybir.AluOpType
 
 P = 128
 PACK = 4
+PAIRS = PACK // 2
 PASSES = K // (P * PACK)
-CHUNKS = ((0, 0, 256), (1, 0, 128), (1, 128, 128))
-FUSED = ((0, 0),)
+QUADRANTS = 4
+LIST_ROWS = 16
+LINE = 4
 HALF = S // 2
 DAMP = 0.6
+OFFSET = 0.2
+
+CHUNKS = ((0, 0, HALF), (1, 0, HALF // 2), (1, HALF // 2, HALF // 2))
+SQUARED_ON_VECTOR = ((0, 1),)
+GATHERED_ON_VECTOR = ((0, 0),)
 
 
-def load_scales(queues, plane, scales):
+def load_scales(nc, plane, scales):
     passes = scales.shape[0]
     rows = plane[:].bitcast(I32).rearrange("p (o n) -> p o n", o=passes)
-    for q in range(4):
-        queues[q].dma_start(
+    for q in range(QUADRANTS):
+        nc.sync.dma_start(
             out=rows[32 * q : 32 * q + 4],
             in_=scales[:, 4 * q : 4 * q + 4, :].bitcast(I32).rearrange("o r n -> r o n"),
         )
+
+
+def load_words(nc, raw, words):
+    nc.sync.dma_start(
+        out=raw[:].bitcast(I32).rearrange("p (o n) -> p o n", o=words.shape[0]),
+        in_=words.bitcast(I32).rearrange("o p n -> p o n"),
+    )
+
+
+def half(h):
+    return slice(h * HALF, (h + 1) * HALF)
+
+
+def entries(list_tile, h):
+    return list_tile[:, h * HALF // LIST_ROWS : (h + 1) * HALF // LIST_ROWS]
 
 
 def tile_picked_ydmpob_psi_p_kernel(
@@ -46,8 +68,8 @@ def tile_picked_ydmpob_psi_p_kernel(
         def sb(shape, dtype, name, tag=None):
             return keep.tile(shape, dtype, name=name, tag=tag or name, align_bytes=64)
 
-        offs_t = keep.tile([P, S // 16], U16, name="offs_t")
-        phs_t = keep.tile([P, S // 16], U16, name="phs_t")
+        offs_t = keep.tile([P, S // LIST_ROWS], U16, name="offs_t")
+        phs_t = keep.tile([P, S // LIST_ROWS], U16, name="phs_t")
         xs = sb([P, PASSES * T], U8, "xs")
         w2s_raw = sb([P, PASSES * H], U8, "w2s_raw")
         w1s_raw = sb([P, PASSES * H], U8, "w1s_raw")
@@ -62,33 +84,28 @@ def tile_picked_ydmpob_psi_p_kernel(
         w2_raw = sb([P, PASSES * 2 * H], U8, "w2_raw")
         w1_raw = sb([P, PASSES * 2 * H], U8, "w1_raw")
         w3w = sb([P, 2 * N], U8, "w3w")
-        ph_t = sb([P, PACK, S], F32, "ph_t")
+        ph_t = [sb([P, 2, S], F32, f"ph{pair}") for pair in range(PAIRS)]
         goal_t = sb([P, PACK, S], F32, "goal_t")
         unit_t = sb([P, PACK], F32, "unit_t")
-
-        def load_words(queue, raw, words):
-            queue.dma_start(
-                out=raw[:].bitcast(I32).rearrange("p (o n) -> p o n", o=words.shape[0]),
-                in_=words.bitcast(I32).rearrange("o p n -> p o n"),
-            )
 
         def load_x(o):
             nc.sync.dma_start(out=xw[o][:].bitcast(I32), in_=x_words[o].rearrange("p c r -> p (c r)").bitcast(I32))
 
         nc.sync.dma_start(offs_t[:], offs)
         load_x(0)
-        load_scales([nc.sync] * 4, xs, x_scales)
+        load_scales(nc, xs, x_scales)
         load_x(1)
-        load_words(nc.sync, w2_raw, w2_words)
-        load_scales([nc.sync] * 4, w2s_raw, w2_scales)
-        nc.sync.dma_start(out=ph_t[:], in_=ph.rearrange("(p t) j -> p t j", t=PACK))
-        load_words(nc.sync, w1_raw, w1_words)
-        load_scales([nc.sync] * 4, w1s_raw, w1_scales)
+        load_words(nc, w2_raw, w2_words)
+        load_scales(nc, w2s_raw, w2_scales)
+        load_words(nc, w1_raw, w1_words)
+        for pair in range(PAIRS):
+            nc.sync.dma_start(out=ph_t[pair][:], in_=ph.rearrange("(p t) j -> p t j", t=PACK)[:, 2 * pair : 2 * pair + 2, :])
+        load_scales(nc, w1s_raw, w1_scales)
         nc.sync.dma_start(out=goal_t[:], in_=goal.rearrange("(p t) j -> p t j", t=PACK))
         nc.sync.dma_start(phs_t[:], phs)
         nc.sync.dma_start(out=unit_t[:], in_=unit.rearrange("(p t) o -> p (t o)", t=PACK))
-        load_words(nc.sync, w3w, w3_words)
-        load_scales([nc.sync] * 4, w3s, w3_scales)
+        load_words(nc, w3w, w3_words)
+        load_scales(nc, w3s, w3_scales)
 
         def deal(words_raw, scales_raw, name, engine):
             words = sb([P, PASSES * 2 * H], U8, name + "_words")
@@ -107,26 +124,22 @@ def tile_picked_ydmpob_psi_p_kernel(
         gw = [sb([P, S], U32, f"gw{o}") for o in range(PASSES)]
         gs = [sb([P, S], U8, f"gs{o}") for o in range(PASSES)]
 
-        def half(h):
-            return slice(h * HALF, (h + 1) * HALF)
-
         def pick(h):
-            entries = offs_t[:, h * HALF // 16 : (h + 1) * HALF // 16]
             for o in range(PASSES):
-                nc.vector.tensor_copy(out=gs[o][:, half(h)], in_=xs[:, o * T : (o + 1) * T].indirect(entries))
+                nc.vector.tensor_copy(out=gs[o][:, half(h)], in_=xs[:, o * T : (o + 1) * T].indirect(entries(offs_t, h)))
             for o in range(PASSES):
-                nc.vector.tensor_copy(out=gw[o][:, half(h)], in_=xw[o][:].indirect(entries))
+                nc.vector.tensor_copy(out=gw[o][:, half(h)], in_=xw[o][:].indirect(entries(offs_t, h)))
 
         pick(0)
         w2w, w2s = deal(w2_raw, w2s_raw, "w2", nc.gpsimd)
         pick(1)
-        w1w, w1s = deal(w1_raw, w1s_raw, "w1", nc.gpsimd)
+        w1w, w1s = deal(w1_raw, w1s_raw, "w1", nc.vector)
 
-        def product(bank, words, scales, t, cols):
+        def product(sums, words, scales, t, cols):
             for o in range(PASSES):
                 c0 = o * H + t * P
                 nc.tensor.matmul_mx(
-                    out=bank,
+                    out=sums,
                     lhsT=words[:, 2 * c0 : 2 * (c0 + P)].bitcast(FP4X4),
                     lhsT_scale=scales[:, c0 : c0 + P],
                     rhs=gw[o][:, cols].bitcast(FP8X4),
@@ -138,16 +151,19 @@ def tile_picked_ydmpob_psi_p_kernel(
         sq = sb([P, PACK, S], F32, "sq", tag="sq_or_root")
         psi, y, damp = [], [], []
 
+        def short_bank(shape, name):
+            return psum.tile(shape, F32, name=name, tag="short", bufs=4)
+
         def distance(pair, h):
             rows = slice(2 * pair, 2 * pair + 2)
-            ww = psum.tile([P, 2, HALF], F32, name="ww", tag="short", bufs=4)
+            ww = short_bank([P, 2, HALF], "ww")
             for u in range(2):
                 product(ww[:, u, :], w2w, w2s, 2 * pair + u, half(h))
             ctr = sb([P, 2, HALF], F32, f"ctr{pair}{h}")
             nc.scalar.activation(ctr[:], ww[:], ACT.Tanh)
             dist = sb([P, 2, HALF], F32, f"dist{pair}{h}")
-            nc.vector.tensor_tensor(dist[:], ctr[:], ph_t[:, rows, half(h)], ALU.subtract)
-            if pair == 0:
+            nc.vector.tensor_tensor(dist[:], ctr[:], ph_t[pair][:, :, half(h)], ALU.subtract)
+            if (pair, h) in SQUARED_ON_VECTOR:
                 nc.vector.tensor_tensor(sq[:, rows, half(h)], dist[:], dist[:], ALU.mult)
             else:
                 nc.scalar.activation(sq[:, rows, half(h)], dist[:], ACT.Square)
@@ -156,7 +172,7 @@ def tile_picked_ydmpob_psi_p_kernel(
             psi_t = sb([P, S + 1], F32, f"psi{t}")
             nc.scalar.activation(psi_t[:, :S], sq[:, t, :], ACT.Exp, scale=-1.0, accum_out=psi_t[:, S:])
             den = sb([P, 1], F32, f"den{t}")
-            nc.vector.tensor_scalar(den[:], psi_t[:, S:], -1.0 / (DAMP * S), -0.2 / DAMP, ALU.mult, ALU.add)
+            nc.vector.tensor_scalar(den[:], psi_t[:, S:], -1.0 / (DAMP * S), -OFFSET / DAMP, ALU.mult, ALU.add)
             damp_t = sb([P, S + 1], F32, f"damp{t}")
             nc.vector.reciprocal(damp_t[:, S:], den[:])
             y_t = psum.tile([P, S], F32, name=f"y{t}", tag=f"y{t}")
@@ -165,26 +181,24 @@ def tile_picked_ydmpob_psi_p_kernel(
             y.append(y_t)
             damp.append(damp_t)
 
-        distance(0, 0)
-        distance(0, 1)
-        gauss(0)
-        gauss(1)
-        distance(1, 0)
-        distance(1, 1)
-        gauss(2)
-        gauss(3)
-
-        def places(h):
-            return phs_t[:, h * HALF // 16 : (h + 1) * HALF // 16]
+        for pair in range(PAIRS):
+            for h in range(2):
+                distance(pair, h)
+            for u in range(2):
+                gauss(2 * pair + u)
 
         acc = sb([P, 2, PACK, HALF], F32, "acc")
         pull = [sb([P, S], F32, f"pull{t}") for t in range(PACK)]
+
+        def accelerate(t, h):
+            nc.vector.tensor_tensor(acc[:, h, t, :], damp[t][:].indirect(entries(phs_t, h)), pull[t][:, half(h)], ALU.add)
+
         for t in range(PACK):
             nc.vector.scalar_tensor_tensor(damp[t][:, :S], y[t][:], damp[t][:, S:], psi[t][:, :S], ALU.mult, ALU.mult)
             nc.vector.scalar_tensor_tensor(pull[t][:], damp[t][:, :S], -1.0 / DAMP, goal_t[:, t, :], ALU.mult, ALU.add)
-            nc.vector.tensor_tensor(acc[:, 0, t, :], damp[t][:].indirect(places(0)), pull[t][:, half(0)], ALU.add)
+            accelerate(t, 0)
         for t in range(PACK):
-            nc.vector.tensor_tensor(acc[:, 1, t, :], damp[t][:].indirect(places(1)), pull[t][:, half(1)], ALU.add)
+            accelerate(t, 1)
 
         root = sb([P, 2, PACK, HALF], F32, "root", tag="sq_or_root")
         mag = sb([P, 2, PACK, HALF], F32, "mag")
@@ -193,11 +207,11 @@ def tile_picked_ydmpob_psi_p_kernel(
         right = sb([P, 2, PACK, HALF], F32, "right")
 
         def saturate(h):
-            for pair in range(2):
+            for pair in range(PAIRS):
                 rows = slice(2 * pair, 2 * pair + 2)
-                fused = (pair, h) in FUSED
+                on_vector = (pair, h) in GATHERED_ON_VECTOR
                 nc.scalar.activation(mag[:, h, rows, :], acc[:, h, rows, :], ACT.Abs)
-                if fused:
+                if on_vector:
                     nc.scalar.activation(root[:, h, rows, :], mag[:, h, rows, :], ACT.Abs_reciprocal_sqrt, bias=one[:])
                 else:
                     nc.scalar.activation(mag2[:, h, rows, :], mag[:, h, rows, :], ACT.Square, bias=one[:])
@@ -206,11 +220,12 @@ def tile_picked_ydmpob_psi_p_kernel(
                     nc.vector.scalar_tensor_tensor(
                         left[:, h, t, :], acc[:, h, t, :], unit_t[:, t : t + 1], root[:, h, t, :], ALU.mult, ALU.mult
                     )
-                    if fused:
-                        nc.vector.tensor_tensor(right[:, h, t, :], psi[t][:].indirect(places(h)), root[:, h, t, :], ALU.mult)
+                    if on_vector:
+                        picked = psi[t][:].indirect(entries(phs_t, h))
+                        nc.vector.tensor_tensor(right[:, h, t, :], picked, root[:, h, t, :], ALU.mult)
             for t in range(PACK):
-                if (t // 2, h) not in FUSED:
-                    nc.scalar.activation(right[:, h, t, :], psi[t][:].indirect(places(h)), ACT.Copy)
+                if (t // 2, h) not in GATHERED_ON_VECTOR:
+                    nc.scalar.activation(right[:, h, t, :], psi[t][:].indirect(entries(phs_t, h)), ACT.Copy)
 
         out_v = out.rearrange("(mt p) j -> p mt j", p=P)
         for c, (h, j0, width) in enumerate(CHUNKS):
@@ -220,22 +235,22 @@ def tile_picked_ydmpob_psi_p_kernel(
             cols = slice(h * HALF + j0, h * HALF + j0 + width)
             hid = sb([P, width * PACK], BF16, f"hid{c}")
             nc.vector.tensor_tensor(
-                hid[:].rearrange("p (g i t) -> p g t i", i=4, t=PACK),
-                left[:, h, :, inner].rearrange("p t (g i) -> p g t i", i=4),
-                right[:, h, :, inner].rearrange("p t (g i) -> p g t i", i=4),
+                hid[:].rearrange("p (g i t) -> p g t i", i=LINE, t=PACK),
+                left[:, h, :, inner].rearrange("p t (g i) -> p g t i", i=LINE),
+                right[:, h, :, inner].rearrange("p t (g i) -> p g t i", i=LINE),
                 ALU.mult,
             )
             codes = sb([P, width], U32, f"codes{c}")
-            plane = sb([P, width], U8, f"plane{c}")
-            nc.vector.quantize_mx(out=codes[:].bitcast(FP8X4), scales=plane[:], in_=hid[:])
-            joints = psum.tile([P, N // P, width], F32, name="joints", tag="short", bufs=4)
+            hid_plane = sb([P, width], U8, f"plane{c}")
+            nc.vector.quantize_mx(out=codes[:].bitcast(FP8X4), scales=hid_plane[:], in_=hid[:])
+            joints = short_bank([P, N // P, width], "joints")
             for mt in range(N // P):
                 nc.tensor.matmul_mx(
                     out=joints[:, mt, :],
                     lhsT=w3w[:, 2 * mt * P : 2 * (mt + 1) * P].bitcast(FP4X4),
                     lhsT_scale=w3s[:, mt * P : (mt + 1) * P],
                     rhs=codes[:].bitcast(FP8X4),
-                    rhs_scale=plane[:],
+                    rhs_scale=hid_plane[:],
                     start=True,
                     stop=True,
                 )

from contextlib import ExitStack

import concourse.mybir as mybir

K, T, S, N, H = 1024, 1024, 512, 256, 512
FLOPS = 2 * S * (2 * K * H + H * N)

F32 = mybir.dt.float32
BF16 = mybir.dt.bfloat16
I32 = mybir.dt.int32
U32 = mybir.dt.uint32
U16 = mybir.dt.uint16
U8 = mybir.dt.uint8
FP8X4 = mybir.dt.float8_e4m3fn_x4
FP4X4 = mybir.dt.float4_e2m1fn_x4
ACT = mybir.ActivationFunctionType
ALU = mybir.AluOpType

P = 128
PACK = 4
PAIRS = PACK // 2
PASSES = K // (P * PACK)
QUADRANTS = 4
LIST_ROWS = 16
LINE = 4
HALF = S // 2
DAMP = 0.6
OFFSET = 0.2

CHUNKS = ((0, 0, HALF), (1, 0, HALF // 2), (1, HALF // 2, HALF // 2))
SQUARED_ON_VECTOR = ((0, 1),)
GATHERED_ON_VECTOR = ((0, 0),)


def load_scales(nc, plane, scales):
    passes = scales.shape[0]
    rows = plane[:].bitcast(I32).rearrange("p (o n) -> p o n", o=passes)
    for q in range(QUADRANTS):
        nc.sync.dma_start(
            out=rows[32 * q : 32 * q + 4],
            in_=scales[:, 4 * q : 4 * q + 4, :].bitcast(I32).rearrange("o r n -> r o n"),
        )


def load_words(nc, raw, words):
    nc.sync.dma_start(
        out=raw[:].bitcast(I32).rearrange("p (o n) -> p o n", o=words.shape[0]),
        in_=words.bitcast(I32).rearrange("o p n -> p o n"),
    )


def half(h):
    return slice(h * HALF, (h + 1) * HALF)


def entries(list_tile, h):
    return list_tile[:, h * HALF // LIST_ROWS : (h + 1) * HALF // LIST_ROWS]


def tile_picked_ydmpob_psi_p_kernel(
    tc, x_words, x_scales, w1_words, w1_scales, w2_words, w2_scales, ph, goal, unit, w3_words, w3_scales, offs, phs, out
):
    nc = tc.nc
    with ExitStack() as ctx:
        keep = ctx.enter_context(tc.tile_pool(name="keep", bufs=1))
        psum = ctx.enter_context(tc.psum_pool(name="psum", bufs=1))

        def sb(shape, dtype, name, tag=None):
            return keep.tile(shape, dtype, name=name, tag=tag or name, align_bytes=64)

        offs_t = keep.tile([P, S // LIST_ROWS], U16, name="offs_t")
        phs_t = keep.tile([P, S // LIST_ROWS], U16, name="phs_t")
        xs = sb([P, PASSES * T], U8, "xs")
        w2s_raw = sb([P, PASSES * H], U8, "w2s_raw")
        w1s_raw = sb([P, PASSES * H], U8, "w1s_raw")
        w3s = sb([P, N], U8, "w3s")
        one = sb([P, 1], F32, "one")
        nc.gpsimd.memset(xs[:].bitcast(I32), 0)
        for plane in (w2s_raw, w1s_raw, w3s):
            nc.vector.memset(plane[:].bitcast(I32), 0)
        nc.vector.memset(one[:], 1.0)

        xw = [sb([P, T], U32, f"xw{o}") for o in range(PASSES)]
        w2_raw = sb([P, PASSES * 2 * H], U8, "w2_raw")
        w1_raw = sb([P, PASSES * 2 * H], U8, "w1_raw")
        w3w = sb([P, 2 * N], U8, "w3w")
        ph_t = [sb([P, 2, S], F32, f"ph{pair}") for pair in range(PAIRS)]
        goal_t = sb([P, PACK, S], F32, "goal_t")
        unit_t = sb([P, PACK], F32, "unit_t")

        def load_x(o):
            nc.sync.dma_start(out=xw[o][:].bitcast(I32), in_=x_words[o].rearrange("p c r -> p (c r)").bitcast(I32))

        nc.sync.dma_start(offs_t[:], offs)
        load_x(0)
        load_scales(nc, xs, x_scales)
        load_x(1)
        load_words(nc, w2_raw, w2_words)
        load_scales(nc, w2s_raw, w2_scales)
        load_words(nc, w1_raw, w1_words)
        for pair in range(PAIRS):
            nc.sync.dma_start(out=ph_t[pair][:], in_=ph.rearrange("(p t) j -> p t j", t=PACK)[:, 2 * pair : 2 * pair + 2, :])
        load_scales(nc, w1s_raw, w1_scales)
        nc.sync.dma_start(out=goal_t[:], in_=goal.rearrange("(p t) j -> p t j", t=PACK))
        nc.sync.dma_start(phs_t[:], phs)
        nc.sync.dma_start(out=unit_t[:], in_=unit.rearrange("(p t) o -> p (t o)", t=PACK))
        load_words(nc, w3w, w3_words)
        load_scales(nc, w3s, w3_scales)

        def deal(words_raw, scales_raw, name, engine):
            words = sb([P, PASSES * 2 * H], U8, name + "_words")
            scales = sb([P, PASSES * H], U8, name + "_scales")
            nc.scalar.copy(
                out=words[:].bitcast(U16).rearrange("p (o t m) -> p o t m", o=PASSES, t=PACK),
                in_=words_raw[:].bitcast(U16).rearrange("p (o m t) -> p o t m", o=PASSES, t=PACK),
            )
            for o in range(PASSES):
                engine.tensor_copy(
                    out=scales[:, o * H : (o + 1) * H].rearrange("p (t m) -> p t m", t=PACK),
                    in_=scales_raw[:, o * H : (o + 1) * H].rearrange("p (m t) -> p t m", t=PACK),
                )
            return words, scales

        gw = [sb([P, S], U32, f"gw{o}") for o in range(PASSES)]
        gs = [sb([P, S], U8, f"gs{o}") for o in range(PASSES)]

        def pick(h):
            for o in range(PASSES):
                nc.vector.tensor_copy(out=gs[o][:, half(h)], in_=xs[:, o * T : (o + 1) * T].indirect(entries(offs_t, h)))
            for o in range(PASSES):
                nc.vector.tensor_copy(out=gw[o][:, half(h)], in_=xw[o][:].indirect(entries(offs_t, h)))

        pick(0)
        w2w, w2s = deal(w2_raw, w2s_raw, "w2", nc.gpsimd)
        pick(1)
        w1w, w1s = deal(w1_raw, w1s_raw, "w1", nc.vector)

        def product(sums, words, scales, t, cols):
            for o in range(PASSES):
                c0 = o * H + t * P
                nc.tensor.matmul_mx(
                    out=sums,
                    lhsT=words[:, 2 * c0 : 2 * (c0 + P)].bitcast(FP4X4),
                    lhsT_scale=scales[:, c0 : c0 + P],
                    rhs=gw[o][:, cols].bitcast(FP8X4),
                    rhs_scale=gs[o][:, cols],
                    start=(o == 0),
                    stop=(o == PASSES - 1),
                )

        sq = sb([P, PACK, S], F32, "sq", tag="sq_or_root")
        psi, y, damp = [], [], []

        def short_bank(shape, name):
            return psum.tile(shape, F32, name=name, tag="short", bufs=4)

        def distance(pair, h):
            rows = slice(2 * pair, 2 * pair + 2)
            ww = short_bank([P, 2, HALF], "ww")
            for u in range(2):
                product(ww[:, u, :], w2w, w2s, 2 * pair + u, half(h))
            ctr = sb([P, 2, HALF], F32, f"ctr{pair}{h}")
            nc.scalar.activation(ctr[:], ww[:], ACT.Tanh)
            dist = sb([P, 2, HALF], F32, f"dist{pair}{h}")
            nc.vector.tensor_tensor(dist[:], ctr[:], ph_t[pair][:, :, half(h)], ALU.subtract)
            if (pair, h) in SQUARED_ON_VECTOR:
                nc.vector.tensor_tensor(sq[:, rows, half(h)], dist[:], dist[:], ALU.mult)
            else:
                nc.scalar.activation(sq[:, rows, half(h)], dist[:], ACT.Square)

        def gauss(t):
            psi_t = sb([P, S + 1], F32, f"psi{t}")
            nc.scalar.activation(psi_t[:, :S], sq[:, t, :], ACT.Exp, scale=-1.0, accum_out=psi_t[:, S:])
            den = sb([P, 1], F32, f"den{t}")
            nc.vector.tensor_scalar(den[:], psi_t[:, S:], -1.0 / (DAMP * S), -OFFSET / DAMP, ALU.mult, ALU.add)
            damp_t = sb([P, S + 1], F32, f"damp{t}")
            nc.vector.reciprocal(damp_t[:, S:], den[:])
            y_t = psum.tile([P, S], F32, name=f"y{t}", tag=f"y{t}")
            product(y_t[:], w1w, w1s, t, slice(0, S))
            psi.append(psi_t)
            y.append(y_t)
            damp.append(damp_t)

        for pair in range(PAIRS):
            for h in range(2):
                distance(pair, h)
            for u in range(2):
                gauss(2 * pair + u)

        acc = sb([P, 2, PACK, HALF], F32, "acc")
        pull = [sb([P, S], F32, f"pull{t}") for t in range(PACK)]

        def accelerate(t, h):
            nc.vector.tensor_tensor(acc[:, h, t, :], damp[t][:].indirect(entries(phs_t, h)), pull[t][:, half(h)], ALU.add)

        for t in range(PACK):
            nc.vector.scalar_tensor_tensor(damp[t][:, :S], y[t][:], damp[t][:, S:], psi[t][:, :S], ALU.mult, ALU.mult)
            nc.vector.scalar_tensor_tensor(pull[t][:], damp[t][:, :S], -1.0 / DAMP, goal_t[:, t, :], ALU.mult, ALU.add)
            accelerate(t, 0)
        for t in range(PACK):
            accelerate(t, 1)

        root = sb([P, 2, PACK, HALF], F32, "root", tag="sq_or_root")
        mag = sb([P, 2, PACK, HALF], F32, "mag")
        mag2 = sb([P, 2, PACK, HALF], F32, "mag2")
        left = sb([P, 2, PACK, HALF], F32, "left")
        right = sb([P, 2, PACK, HALF], F32, "right")

        def saturate(h):
            for pair in range(PAIRS):
                rows = slice(2 * pair, 2 * pair + 2)
                on_vector = (pair, h) in GATHERED_ON_VECTOR
                nc.scalar.activation(mag[:, h, rows, :], acc[:, h, rows, :], ACT.Abs)
                if on_vector:
                    nc.scalar.activation(root[:, h, rows, :], mag[:, h, rows, :], ACT.Abs_reciprocal_sqrt, bias=one[:])
                else:
                    nc.scalar.activation(mag2[:, h, rows, :], mag[:, h, rows, :], ACT.Square, bias=one[:])
                    nc.scalar.activation(root[:, h, rows, :], mag2[:, h, rows, :], ACT.Abs_reciprocal_sqrt)
                for t in (2 * pair, 2 * pair + 1):
                    nc.vector.scalar_tensor_tensor(
                        left[:, h, t, :], acc[:, h, t, :], unit_t[:, t : t + 1], root[:, h, t, :], ALU.mult, ALU.mult
                    )
                    if on_vector:
                        picked = psi[t][:].indirect(entries(phs_t, h))
                        nc.vector.tensor_tensor(right[:, h, t, :], picked, root[:, h, t, :], ALU.mult)
            for t in range(PACK):
                if (t // 2, h) not in GATHERED_ON_VECTOR:
                    nc.scalar.activation(right[:, h, t, :], psi[t][:].indirect(entries(phs_t, h)), ACT.Copy)

        out_v = out.rearrange("(mt p) j -> p mt j", p=P)
        for c, (h, j0, width) in enumerate(CHUNKS):
            if j0 == 0:
                saturate(h)
            inner = slice(j0, j0 + width)
            cols = slice(h * HALF + j0, h * HALF + j0 + width)
            hid = sb([P, width * PACK], BF16, f"hid{c}")
            nc.vector.tensor_tensor(
                hid[:].rearrange("p (g i t) -> p g t i", i=LINE, t=PACK),
                left[:, h, :, inner].rearrange("p t (g i) -> p g t i", i=LINE),
                right[:, h, :, inner].rearrange("p t (g i) -> p g t i", i=LINE),
                ALU.mult,
            )
            codes = sb([P, width], U32, f"codes{c}")
            hid_plane = sb([P, width], U8, f"plane{c}")
            nc.vector.quantize_mx(out=codes[:].bitcast(FP8X4), scales=hid_plane[:], in_=hid[:])
            joints = short_bank([P, N // P, width], "joints")
            for mt in range(N // P):
                nc.tensor.matmul_mx(
                    out=joints[:, mt, :],
                    lhsT=w3w[:, 2 * mt * P : 2 * (mt + 1) * P].bitcast(FP4X4),
                    lhsT_scale=w3s[:, mt * P : (mt + 1) * P],
                    rhs=codes[:].bitcast(FP8X4),
                    rhs_scale=hid_plane[:],
                    start=True,
                    stop=True,
                )
            res = sb([P, N // P, width], F32, f"res{c}")
            nc.scalar.copy(res[:], joints[:])
            nc.sync.dma_start(out=out_v[:, :, cols], in_=res[:])
